import numpy as np, ml_dtypes
CORES = [5,29,101,125,133,157,229,253]
N = 8
BF = ml_dtypes.bfloat16
def gentries(a):
    return np.ascontiguousarray(a.reshape(8, 16, -1).transpose(0, 2, 1)).reshape(8, -1)
def gtable(e):
    e = np.asarray(e); return np.ascontiguousarray(e.reshape(8, -1, 16).transpose(0, 2, 1)).reshape(128, -1).astype(np.int32)
V, X, SW, RO, CAP = 512, 80, 2, 3, 40
E = (N - 1) * X
Q = 4 ** SW
def base(rng, top):
    b = rng.integers(top // 10, top * 9 // 10, (N, 8, 1, V))
    debt = np.clip(b + rng.integers(-(top // 16), top // 16 + 1, (N, 8, 16, V)), 1, top)
    c = rng.integers(1, top // 5 + 1, (N, 8, 1, 4 * V)); few = rng.random((N, 8, 1, 4 * V)) < 0.5
    coll = np.where(few, 0, np.clip(c + rng.integers(-16, 17, (N, 8, 16, 4 * V)), 0, top // 5))
    o = np.argsort(rng.random((N, 8, 4 * V)), axis=-1)
    rest = np.concatenate([o[..., E:], np.broadcast_to(4 * V + np.arange(E), (N, 8, E))], axis=-1)
    sg = np.take_along_axis(rest, np.argsort(rng.random((N, 8, 4 * V)), axis=-1), 2)
    return {"cash": rng.integers(0, top // 8 + 1, (N, 8, 16, V)), "debt": debt, "coll": coll, "sg": sg, "xp": np.ascontiguousarray(o[..., :E]),
            "th": Q + rng.integers(0, Q // 4 + 1, (N, 8, 16)), "val": real(rng, 0)}
def real(rng, w):
    s = np.exp2(rng.integers(-w, w + 1, (N, 8, 1, V)))
    return (s * (0.5 + rng.random((N, 8, 16, V)))).astype(np.float32)
def lay(rng, S, C, F, at=None):
    S = np.asarray(S, np.int64).reshape(-1); C = np.asarray(C, np.int64).reshape(-1); F = np.asarray(F, np.int64).reshape(-1)
    left = rng.permutation(np.setdiff1d(np.arange(4 * V), np.concatenate([C, F]))); m = E - len(F)
    x = np.full(E, -1, np.int64); x[rng.permutation(E)[:len(F)] if at is None else at] = F; x[x < 0] = left[:m]
    s = np.full(4 * V, -1, np.int64); s[S] = C
    s[s < 0] = rng.permutation(np.concatenate([left[m:], np.setdiff1d(4 * V + np.arange(E), C)]))
    return s, x
def four_of(b):
    return (4 * np.asarray(b, np.int64)[:, None] + np.arange(4)).reshape(-1)
def pack(d):
    return {"cash": d["cash"].reshape(N, 128, V).astype(np.int32), "debt": d["debt"].reshape(N, 128, V).astype(np.int32),
            "coll": d["coll"].reshape(N, 128, 4 * V).astype(np.float32).astype(BF), "sig": np.stack([gtable(a) for a in d["sg"]]),
            "xpt": np.stack([gtable(a) for a in d["xp"]]), "th": d["th"].reshape(N, 128, 1).astype(np.int32), "val": np.ascontiguousarray(d["val"].reshape(N, 128, V)).astype(np.float32)}
def setup_inputs(rng):
    return pack(base(rng, 1000))
def setup_inputs_spread(rng):
    d = base(rng, 1000); one = (N, 8, 1, V); full = (N, 8, 16, V)
    b = np.where(rng.random(one) < 0.5, np.exp2(10 * rng.random(one)), 1 + 1023 * rng.random(one))
    d["debt"] = np.clip((b * (0.75 + 0.5 * rng.random(full))).astype(np.int64), 1, 1023)
    d["cash"] = np.clip((np.exp2(10 * rng.random(one) ** 2) * rng.random(full)).astype(np.int64), 0, 1023)
    c = np.exp2(8 * rng.random((N, 8, 1, 4 * V))) * (rng.random((N, 8, 1, 4 * V)) < 0.5)
    d["coll"] = np.clip((c * rng.random((N, 8, 16, 4 * V))).astype(np.int64), 0, 255)
    d["th"] = Q + (SW * Q * rng.random((N, 8, 16)) ** 4).astype(np.int64)
    d["val"] = 32.0 * real(rng, 1)
    return pack(d)
def setup_inputs_ends(rng):
    d = base(rng, 1000); full = (N, 8, 16, V)
    z = np.where(rng.random((N, 8, 1, V)) < 0.5, rng.random((N, 8, 1, V)), rng.random(full))
    d["cash"] = np.where(z < 0.8, 0, 1023); d["debt"] = np.where((z < 0.6) | (z > 0.87), 1023, 1)
    c = np.where(rng.random((N, 8, 1, 4 * V)) < 0.5, rng.random((N, 8, 1, 4 * V)), rng.random((N, 8, 16, 4 * V)))
    d["coll"] = np.where(c < 0.25, 255, 0)
    d["val"] = np.where(rng.random(full) < 0.75, 128.0, 8.0)
    n = rng.choice(np.array([0, 8, 9, 16]), (N, 8, 1)); n[:, 0] = 16; n[:, 1] = 9; n[:, 2] = 8; n[:, 7] = 0
    d["th"] = np.where(np.argsort(rng.random((N, 8, 16)), axis=-1) < n, Q, Q * (1 + SW))
    slots = [np.concatenate([np.array([0, E - 1]), 1 + rng.permutation(E - 2)[:8 * RO - 2]]) for j in range(4)]
    top = np.concatenate([4 * np.array([0, 1, V // 4 - 2, V // 4 - 1]) + 3 - t for t in range(RO)])
    b = 4 * np.arange(V // 4); inner = b[(4 * b >= E // 2) & (4 * b + 3 < 4 * V - (E - E // 2))]
    for q in range(N):
        for g in range(8):
            at = slots[(g - 1) // 2]; S = []; C = []; T = []; hold = []; i = 0; k = 4 * RO
            if g % 2:
                more = rng.permutation(b); feed = (4 * top[:, None] + np.arange(2)).reshape(-1); F = feed + 2; T.append(top); hold.append(four_of(top))
            else:
                more = rng.permutation(inner); feed = 4 * V + at; F = np.concatenate([np.arange(E // 2), np.arange(4 * V - (E - E // 2), 4 * V)])
            for j in range(SW):
                nxt = more[i:i + k]; i += k; k *= 2
                S.append((4 * nxt[:, None] + np.arange(2)).reshape(-1)); C.append(feed); feed = four_of(nxt)
                T.append(nxt); hold.append((4 * nxt[:, None] + np.arange(2, 4)).reshape(-1))
            T = np.concatenate(T); hold = np.concatenate(hold); leak = more[i:i + len(hold) // 4]
            S.append(hold); C.append(four_of(leak))
            d["sg"][q, g], d["xp"][q, g] = lay(rng, np.concatenate(S), np.concatenate(C), F, at if g % 2 else None)
            d["cash"][q, g][:, T] = 0; d["debt"][q, g][:, T] = 1023; d["coll"][q, g][:, four_of(T)] = 0; d["val"][q, g][:, T] = 128.0
            d["cash"][q, g][:, leak] = 0; d["debt"][q, g][:, leak] = 1
    return pack(d)
def setup_inputs_corners(rng):
    d = base(rng, 600); d["debt"] = d["debt"] & -4
    d["val"] = ((2 ** 16 + rng.integers(0, 2 ** 14, (N, 8, 16, V)) + 0.4921875) * 2.0 ** -20).astype(np.float32)
    d["th"][:] = Q; d["th"][:, 3::4] = Q * (1 + SW)
    for q in range(N):
        for g in range(8):
            cash, debt, coll = d["cash"][q, g], d["debt"][q, g], d["coll"][q, g]
            S = []; C = []; F = []; vs = []; h = 4 * rng.permutation(V // 4)
            for t in range(RO):
                i = np.sort(np.concatenate([np.array([0]), 1 + rng.permutation(V // 4 - 2)[:10], np.array([V // 4 - 1])]))
                v = 4 * i + 3 - t; u = h[8 * t:8 * t + 8]; vs.append(v)
                S += [4 * v[1] + 1, 4 * v[2] + 1, 4 * u[0] + 2, 4 * u[1], 4 * u[1] + 3, 4 * v[5] + 2, 4 * u[2] + 1, 4 * u[3] + 1, 4 * u[4] + 1, 4 * u[5] + 1, 4 * v[9] + 3 if g % 2 == 0 else 4 * u[6]]
                C += [4 * v[j] for j in (0, 1, 2, 3, 4, 5, 7, 8, 9, 10, 11)]; F.append(4 * v[6])
            o1, o2, leak = h[32], h[33], h[34]
            S += [4 * o1 + j for j in range(4)] + [4 * o2 + j for j in range(4)]
            C += [4 * o1, 4 * o1 + 1, 4 * o1 + 2, 4 * leak, 4 * o2, 4 * o2 + 1, 4 * o2 + 2, 4 * o1 + 3]
            d["sg"][q, g], d["xp"][q, g] = lay(rng, S, C, F)
            if g % 2:
                s = d["sg"][q, g]; own = np.flatnonzero((s < 4 * V) & (rng.random(4 * V) < 0.25))
                coll[:, own] = (debt[:, s[own] >> 2] >> 2) - rng.integers(0, 2, (16, len(own)))
            for v in vs:
                cash[:, v] = 0; debt[:, v] = 1023
                cash[rng.permutation(16)[:8], v[7]] = 1023; cash[rng.permutation(16)[:7], v[8]] = 1023
                coll[:, 4 * v[9] + np.arange(4)] = 200; coll[:, 4 * v[10] + np.arange(4)] = np.array([0, 0, 0, 200])
            b = h[24:32]; c = rng.integers(0, 21, (16, 8))
            cash[:, b] = c; debt[:, b] = 800 + c + rng.integers(0, 2, (16, 8)); coll[:, four_of(b)] = 200
            cash[:, h[32:35]] = 0; debt[:, h[32:34]] = 1023; debt[:, leak] = 1; coll[:, four_of(h[32:34])] = 0
    return pack(d)
def setup_inputs_crowd(rng):
    d = base(rng, 600); d["th"][:] = Q; d["th"][:, 3] = Q + rng.integers(0, Q // 4 + 1, (N, 16)); n = V // 32
    for q in range(N):
        for g in range(8):
            cash, debt, coll = d["cash"][q, g], d["debt"][q, g], d["coll"][q, g]; h = 4 * rng.permutation(V // 4); S = []; C = []; lane = rng.permutation(16)
            for t in range(RO):
                v = 4 * rng.permutation(V // 4)[:4 * n] + 3 - t; w = h[t * n:(t + 1) * n]
                S.append(four_of(w)); C.append(4 * v)
                cash[:, v] = 0; debt[:, v] = 1023
                coll[:, 4 * v] = 0; coll[:, 4 * v + 1] = 200; coll[:, 4 * v + 2] = 200; coll[:, 4 * v + 3] = 0; coll[lane[0], 4 * v + 1] = 0
                if g % 2: cash[lane[1], v] = 1023
                cash[:, v.reshape(n, 4)[::2, 3]] = 1023
            d["sg"][q, g], d["xp"][q, g] = lay(rng, np.concatenate(S), np.concatenate(C), [])
    return pack(d)
def setup_inputs_calm(rng):
    d = base(rng, 600)
    n = 9 + rng.integers(0, 8, (N, 8, 1)); d["th"] = np.where(np.argsort(rng.random((N, 8, 16)), axis=-1) < n, Q, Q + rng.integers(0, SW * Q + 1, (N, 8, 16)))
    for q in range(N):
        for g in range(8):
            cash, debt, coll = d["cash"][q, g], d["debt"][q, g], d["coll"][q, g]; h = 4 * rng.permutation(V // 4); S = []; C = []; at = 0
            for t in range(RO):
                k = (g + q + t) % 4 if g < 6 else (0 if t < RO - 1 else V // 4 - (g - 6))
                i = 4 * rng.permutation(V // 4) + 3 - t; v = i[:k]; rest = i[k:]; w = h[at:at + k]; at += k
                m = np.argsort(rng.random((16, len(rest))), axis=0) < 8
                cash[:, rest] = np.where(m, 1023, cash[:, rest])
                c = rng.integers(0, 21, (16, k)); cash[:, v] = c; debt[:, v] = 800 + c + CAP + rng.integers(0, 2, (16, k)); coll[:, four_of(v)] = 200
                S += [4 * w + 3, 4 * v + 1, 4 * v + 2]; C += [4 * v, 4 * w + 1, 4 * w + 2]
                if g >= 6 and t == RO - 1:
                    z = np.concatenate([4 * v, 4 * w])[:E]; S.append(z); C.append(4 * V + rng.permutation(E)[:len(z)])
            d["sg"][q, g], d["xp"][q, g] = lay(rng, np.concatenate(S), np.concatenate(C), [])
    return pack(d)
def check_ranges(d):
    bad = []
    for k, lo, hi in (("cash", 0, 1023), ("debt", 1, 1023), ("coll", 0, 255), ("sig", 0, 4 * V + E - 1), ("xpt", 0, 4 * V - 1), ("th", Q, Q * (1 + SW))):
        a = np.asarray(d[k]).astype(np.float64)
        if not (np.min(a) >= lo and np.max(a) <= hi): bad.append("range of " + k)
        elif np.any(a != np.floor(a)): bad.append("whole numbers of " + k)
    x = np.asarray(d["val"]).astype(np.float64)
    if not (np.min(x) >= 2.0 ** -4 and np.max(x) <= 128): bad.append("range of val")
    elif np.max(x) > 16 * np.min(x): bad.append("uneven sizes of val")
    for q in range(N):
        both = np.sort(np.concatenate([gentries(np.asarray(d["sig"][q])), gentries(np.asarray(d["xpt"][q]))], axis=1), axis=1)
        if np.any(both != np.arange(4 * V + E)[None, :]): bad.append("sig and xpt of rank " + str(q) + " are not every number once")
    return bad
def take(a, i):
    return np.take_along_axis(a, i[:, :, None, :], 3)
def four(y):
    return ((y[..., 0::4] + y[..., 1::4]) + y[..., 2::4]) + y[..., 3::4]
def forth(a):
    out = np.empty_like(a)
    for q in range(N):
        for d in range(1, N):
            b = slice((d - 1) * X, d * X); out[(q + d) % N, :, :, b] = np.roll(a[q, :, :, b], 1, axis=0)
    return out
def home(a):
    out = np.empty_like(a)
    for q in range(N):
        for d in range(1, N):
            b = slice((d - 1) * X, d * X); out[q, :, :, b] = np.roll(a[(q + d) % N, :, :, b], -1, axis=0)
    return out
def clear(e, L, c, sg, xp):
    at = np.where(sg < 4 * V, sg >> 2, sg - 3 * V); p = L
    for k in range(SW):
        y = np.maximum(0.25 * take(np.concatenate([p, forth(take(p, xp >> 2))], axis=3), at), c)
        p = np.minimum(L, e + four(y))
    return p, p < L, y > c
def inverse(sg, xp):
    inv = np.zeros((N, 8, 4 * V + E), np.int64)
    np.put_along_axis(inv, sg, np.arange(4 * V)[None, None, :], 2); np.put_along_axis(inv, xp, 4 * V + np.arange(E)[None, None, :], 2)
    return inv
def threat(D, M, inv, a):
    m = np.where(D, a, 0.0)
    for k in range(SW):
        c = np.where(M, np.repeat(m, 4, axis=3), 0.0)
        z = take(np.concatenate([c, home(take(c, inv[:, :, 4 * V:]))], axis=3), inv[:, :, :4 * V])
        m = np.where(D, a + 0.25 * four(z), 0.0)
    return m
def novate(t, m, M, e, sg, inv, lim):
    v = np.arange(3 - t, V, 4); votes = np.sum(Q * m[..., v] >= lim, axis=2)
    s = inv[:, :, 4 * v]; w = s >> 2; act = (votes >= 9) & (s < 4 * V) & (w != v)
    k = np.argmax(np.sum(~M.reshape(N, 8, 16, V, 4)[:, :, :, v], axis=2), axis=3)
    low = np.full((N, 8, V), V, np.int64); r, g, i = np.nonzero(act)
    low[r, g, v[i]] = v[i]; np.minimum.at(low, (r, g, w[r, g, i]), v[i])
    ok = (low[r, g, v[i]] == v[i]) & (low[r, g, w[r, g, i]] == v[i])
    r, g, i = r[ok], g[ok], i[ok]; e = np.array(e); sg = np.array(sg)
    e[r, g, :, v[i]] += CAP
    a = 4 * v[i] + k[r, g, i]; b = 4 * w[r, g, i] + k[r, g, i]
    sg[r, g, a], sg[r, g, b] = sg[r, g, b], sg[r, g, a]
    return e, sg
def reference(cash, debt, coll, sig, xpt, th, val):
    e = cash.astype(np.float64).reshape(N, 8, 16, V); L = debt.astype(np.float64).reshape(N, 8, 16, V)
    c = coll.astype(np.float32).astype(np.float64).reshape(N, 8, 16, 4 * V); lim = th.astype(np.float64).reshape(N, 8, 16, 1)
    sg = np.stack([gentries(a) for a in sig]).astype(np.int64); xp = np.stack([gentries(a) for a in xpt]).astype(np.int64)
    for t in range(RO):
        p, D, M = clear(e, L, c, sg, xp); inv = inverse(sg, xp)
        e, sg = novate(t, threat(D, M, inv, 1.0), M, e, sg, inv, lim)
    p, D, M = clear(e, L, c, sg, xp)
    m = threat(D, M, inverse(sg, xp), val.astype(np.float64).reshape(N, 8, 16, V))
    return {"pay": p.reshape(N, 128, V).astype(np.float32), "mu": m.reshape(N, 128, V).astype(np.float32)}

def check_inputs(d):
    bad = list(check_ranges(d))
    if not bad:
        for name, y in reference(**d).items():
            for q in range(N):
                v = np.abs(np.asarray(y[q], np.float64)); s = np.sqrt(np.mean(v * v))
                if v.max() > 7 * s or s < 2.0 ** -5: bad.append('%s of rank %d is uneven or too small' % (name, q))
    return bad

from concourse.bass import DstId, RemoteDMATransfer
from concourse.mybir import dt, AluOpType, ActivationFunctionType
A = AluOpType
F = ActivationFunctionType
N, V, X, RO = 8, 512, 80, 3
E = (N - 1) * X
NX = 1 + 3 * (RO + 1)
f32, f16, b16, i32, u16 = "float32", "float16", "bfloat16", "int32", "uint16"
SB_ = {
    "dbf": (512, i32), "db": (512, i32), "csh": (512, i32), "col": (2048, b16), "src": (164, i32), "thi": (8, i32),
    "vl": (512, f32), "vlb": (528, f32),
    "it": (160, i32), "it2": (160, i32), "it3": (256, i32), "io": (992, f32), "io2": (528, f32), "irow": (128, f32),
    "ncol": (8, f32), "thc": (8, f32), "zt": (164, f32),
    "W1f": (160, f32), "Wqf": (160, f32), "W1": (160, b16), "Wn": (160, b16), "Wq": (160, b16), "Wnq": (160, b16),
    "W4": (160, b16), "Wk": (160, b16), "B1f": (160, f32), "B1": (160, b16), "Bn2": (160, b16), "Bk": (160, b16),
    "Bk32": (160, b16), "mk": (256, f32), "mneg": (128, b16), "sgx": (128, b16), "sgn": (128, f32), "sg1": (256, f32),
    "tri": (16, b16),
    "cp": (2048, b16), "L16": (512, f16), "e16": (512, f16), "Lw": (1072, f32), "xw": (1072, f32), "S1f": (768, f32),
    "y": (2048, f16), "xg": (1024, f16), "Dn": (544, b16), "m1b": (544, b16), "m1u": (544, b16),
    "m1f": (528, f32), "z": (2048, b16), "zs": (2048, b16), "zf": (2048, f32), "zsf": (2048, f32), "tf": (512, f32),
    "sigr": (2304, f32), "invA": (2608, f32), "invB": (2864, f32), "ok40": (384, b16),
    "cW": (560, b16), "MW": (560, b16), "vW": (560, f32), "c01w": (560, b16), "res": (512, f32), "res2": (512, f32),
    "xfU": (36, u16), "atU": (128, u16), "spU": (164, u16), "poU": (128, u16), "wcU": (36, u16), "wbU": (36, u16),
    "alU": (32, u16), "ahU": (32, u16), "abU": (16, u16), "sgU": (16, u16), "aaU": (16, u16), "wU": (8, u16),
    "ofU": (16, u16), "ouU": (32, u16),
    "j1": (164, i32), "j2": (164, i32), "g1": (164, f32), "g2": (164, f32), "g3": (164, f32), "g4": (164, f32),
    "wrS": (128, f32), "wrP": (128, f32), "wrP2": (128, f32), "wWp": (36, f32),
    "sg": (512, b16), "kt": (512, f32), "kt2": (256, f32), "key": (128, i32), "kk": (128, i32), "kw": (128, f32),
    "wc": (8, f32), "wcl": (8, f32), "vc": (8, f32), "Em": (128, f32), "Wr": (128, f16), "Vr": (128, f16),
    "en1": (128, b16), "en2": (128, b16), "vb": (256, f32), "vals": (256, f32), "abb": (16, f32), "ab": (16, i32),
    "s1": (16, i32), "s2": (16, f32), "s3": (16, f32), "sgm": (16, f32), "AB": (256, f32), "ABm": (256, f32),
    "ABs": (256, f32), "ci": (16, i32), "spo": (16, i32), "Xv": (256, f16), "cab": (256, b16), "rl": (512, f16),
    "S1w": (256, f32), "nv": (256, f32), "bf": (16, f32), "tb": (1728, b16), "Bp": (576, b16), "tmp": (576, b16),
    "zl": (512, b16), "zg": (512, b16), "vote": (128, b16), "cw": (128, f32), "scw": (128, f32), "o1": (16, f32),
    "o2": (32, f32), "ng": (16, f32), "td": (1152, b16), "ub": (32, f32),
    "exh": (5 * E, f16), "exb": (6 * E, b16), "exf": (2 * E, f32), "lnd": (5 * E, f16),
    "c0": (2608, b16), "c1": (2608, b16), "c2": (2608, b16), "c3": (2048, b16),
    "h0": (576, b16), "h1": (576, b16), "h2": (576, b16), "cf0": (2608, f32), "cf1": (2608, f32),
    "rlh": (5 * X, f16), "rlb": (6 * X, b16), "rlf": (2 * X, f32),
}
ALIAS = {"zf": "invA", "zsf": "sigr", "c3": "zs", "res": "io"}
for _k in ALIAS:
    del SB_[_k]
OWN = ["dbf", "vlb", "rlh", "rlb", "rlf", "h0", "h1", "h2"]
PLACE = {}
SCRATCH = {}
_top = {}
for _k, (_w, _d) in SB_.items():
    if _w > 600 or _k in OWN:
        SCRATCH[_k] = ("sbuf", [128, _w], _d)
        PLACE[_k] = (_k, 0, _w)
    else:
        _at = _top.get(_d, 0)
        PLACE[_k] = ("all" + _d, _at, _w)
        _top[_d] = _at + (_w + 15) // 16 * 16
for _d, _w in _top.items():
    SCRATCH["all" + _d] = ("sbuf", [128, _w], _d)
SCRATCH["xf3"] = ("sbuf", [128, N - 1, 5], i32)
SCRATCH["wW3"] = ("sbuf", [128, N - 1, 5], f32)
SCRATCH["wX3"] = ("sbuf", [128, N - 1, 5], f32)
PS = ["q0", "q1", "q2", "q3", "sA", "sB", "pX", "pY"]
for _k in PS:
    SCRATCH[_k] = ("psum", [128, 512], f32)
DS = ["l%d" % i for i in range(9)] + ["dz", "du", "dS", "dP", "dW", "dP2", "dW2", "dU", "st1", "st2"]
SEMAPHORES = ["sv", "sa", "sp", "sg", "snt"] + DS + ["ar%d" % i for i in range(NX)] + ["ad%d" % i for i in range(NX)]


def routes(T, topo):
    c = T.cores
    rel = [d for d in range(1, N) if not topo.may_write(c[0], c[d])]
    for q in range(N):
        for s in (1, -1):
            assert rel == [d for d in range(1, N) if not topo.may_write(c[q], c[(q + s * d) % N])]
    return rel, [d for d in range(1, N) if d not in rel]


def helper_of(T, topo, q, k, rel):
    c = T.cores[q]
    hs = [h for h in topo.cores_of(c) if h != c and all(
        topo.may_write(h, T.cores[(q + s * d) % N]) for d in rel for s in (1, -1))]
    return hs[k]


def exchanges(rel, dirc):
    order = rel + dirc
    ex = []
    for i in range(5):
        ex.append((1, "exh", i * E, "rlh", i * X, "lnd", {d: i * E + X * order.index(d) for d in order}))
    out = [ex[0]]
    for t in range(RO + 1):
        out.append(ex[t + 1])
        if t < RO:
            out.append((-1, "exb", 2 * t * E, "rlb", 2 * t * X, "c%d" % t, {d: 2048 + X * (d - 1) for d in order}))
            out.append((-1, "exb", (2 * t + 1) * E, "rlb", (2 * t + 1) * X, "h%d" % t, {d: 16 + X * (d - 1) for d in order}))
        else:
            for j in range(2):
                out.append((-1, "exf", j * E, "rlf", j * X, "cf%d" % j, {d: 2048 + X * (d - 1) for d in order}))
    return out


def bits(es):
    m = 0
    for e in es:
        m |= 1 << e
    return m


def helper_program(g, core, T, topo, q, k, rel, dirc):
    d = rel[k]
    sent = 0
    per = len(topo.engines(T.cores[q], core)) // len(rel)
    for x, (s, _sb, _sc, rb, rc, lb, lc) in enumerate(exchanges(rel, dirc)):
        dst = T.cores[(q + s * d) % N]
        rid, pid = topo.addr(dst, core)
        g.wait_ge(T.sem["ar%d" % x], per)
        g.remote_dma(T[lb][:, lc[d]:lc[d] + X], T[rb][:, rc:rc + X], T.sem["ar%d" % x], T.sem.snt, pid, rid,
                     topo.mask(core, dst))
        sent += len(topo.engines(core, dst))
    g.wait_ge(T.sem.snt, sent)


def rank_program(g, core, T, topo):
    rank = T.rank_of(core)
    if rank is None:
        near = [q for q in range(N) if core in topo.cores_of(T.cores[q])]
        if near:
            rel, dirc = routes(T, topo)
            for k in range(len(rel)):
                if helper_of(T, topo, near[0], k, rel) == core:
                    helper_program(g, core, T, topo, near[0], k, rel, dirc)
        return
    rel, dirc = routes(T, topo)
    seq = build(g, core, T, topo, rank, rel, dirc, None)
    stops, nxt = [], {}
    for bank, start in reversed(seq):
        stops.append(nxt.get(bank, True))
        nxt[bank] = start
    build(g, core, T, topo, rank, rel, dirc, stops[::-1])


def build(g, core, T, topo, rank, rel, dirc, stops):
    live = stops is not None
    seq = []
    EX = exchanges(rel, dirc)
    order = rel + dirc
    NR = X * len(rel)
    CR = NR // 16
    assert CR % 2 == 0

    def prog(ds):
        st = ds[1] - ds[0]
        assert all(b - a == st for a, b in zip(ds, ds[1:]))
        return slice(ds[0] - 1, ds[-1], st)
    srel, sdir = prog(rel), prog(dirc)

    Q = {"v": g.vector, "a": g.scalar, "p": g.tensor, "g": g, "s": g.sync}
    SEM = {"v": "sv", "a": "sa", "p": "sp", "g": "sg"}
    cnt = {}
    seen = {e: {} for e in Q}
    snap = {}
    log = {}

    def R(name, a=0, b=None, st=1, ap=None):
        name = ALIAS.get(name, name)
        tn, at, w = PLACE.get(name, (name, 0, 512 if name in PS else 35))
        if b is None:
            b = w
        if ap is None:
            ap = T[tn][:, at + a:at + b] if st == 1 else T[tn][:, at + a:at + b:st]
        return {"ap": ap, "r": [(name, a, b, st)]}

    def G(win, off):
        return {"ap": win["ap"].indirect(off["ap"]), "r": win["r"], "o": off["r"]}

    def wait(e, tok):
        s, n = tok
        if seen[e].get(s, 0) >= n:
            return
        if live:
            Q[e].wait_ge(T.sem[s], n)
        seen[e][s] = n
        for k2, n2 in snap.get(tok, {}).items():
            if seen[e].get(k2, 0) < n2:
                seen[e][k2] = n2

    def deps(e, outs, ins):
        acc = []
        for o in outs:
            acc += [(r, True) for r in o["r"]] + [(r, False) for r in o.get("o", [])]
        for o in ins:
            acc += [(r, False) for r in o["r"] + o.get("o", [])]
        need = {}
        for (nm, a, b, st), w in acc:
            ps = nm in PS
            for (a2, b2, w2, e2, tok, st2) in log.get(nm, []):
                if e == "p" and e2 == "p":
                    continue
                apart = st > 1 and st == st2 and (a - a2) % st != 0
                if (ps and e2 != e) or ((w or w2) and a < b2 and a2 < b and not apart):
                    need[tok[0]] = max(need.get(tok[0], 0), tok[1])
        for s, n in need.items():
            wait(e, (s, n))
        return acc

    def note(e, acc, tok, q=None):
        snap[tok] = dict(seen[q or e])
        for (nm, a, b, st), w in acc:
            lg = log.setdefault(nm, [])
            if w and st == 1 and e != "dma":
                lg[:] = [x for x in lg if not (a <= x[0] and x[1] <= b)]
            lg.append((a, b, w, e, tok, st))

    def do(e, outs, ins, fn):
        acc = deps(e, outs, ins)
        s = SEM[e]
        cnt[s] = cnt.get(s, 0) + 1
        if live:
            fn().then_inc(T.sem[s], 1)
        note(e, acc, (s, cnt[s]))

    def isr(x):
        return isinstance(x, dict)

    def val_(x):
        return x["ap"] if isr(x) else x

    def ts(o, i, s1, op0, s2=None, op1=None):
        ins = [i] + [x for x in (s1, s2) if isr(x)]
        if op1 is None:
            do("v", [o], ins, lambda: g.vector.tensor_scalar(o["ap"], i["ap"], val_(s1), None, op0))
        else:
            do("v", [o], ins, lambda: g.vector.tensor_scalar(o["ap"], i["ap"], val_(s1), val_(s2), op0, op1))

    def tt(o, i, j, op):
        do("v", [o], [i, j], lambda: g.vector.tensor_tensor(o["ap"], i["ap"], j["ap"], op))

    def cp(o, i):
        do("v", [o], [i], lambda: g.vector.tensor_copy(o["ap"], i["ap"]))

    def ms(o, c):
        do("v", [o], [], lambda: g.vector.memset(o["ap"], c))

    def scan(o, d0, d1, op0, op1):
        do("v", [o], [d0, d1], lambda: g.vector.tensor_tensor_scan(o["ap"], d0["ap"], d1["ap"], 0.0, op0, op1))

    def act(o, i, f=F.Copy, bias=0.0, scale=1.0):
        ins = [i] + [x for x in (bias, scale) if isr(x)]
        if f == F.Silu:
            do("a", [o], ins, lambda: g.scalar.activation(o["ap"], i["ap"], f))
        else:
            do("a", [o], ins, lambda: g.scalar.activation(o["ap"], i["ap"], f, bias=val_(bias), scale=val_(scale)))

    def mm(o, w, r, start=False):
        stop = live and stops[len(seq)]
        seq.append((o["r"][0][0], start))
        do("p", [o], [w, r], lambda: g.tensor.matmul(o["ap"], w["ap"], r["ap"], start, stop))

    def iota(o, pat, base, cm, fl=False):
        if fl:
            do("g", [o], [], lambda: g.iota(o["ap"], pat, base, cm, allow_small_or_imprecise_dtypes=True))
        else:
            do("g", [o], [], lambda: g.iota(o["ap"], pat, base, cm))

    def dmas(e, s, pairs):
        accs = []
        for o, i in pairs:
            accs += deps(e, [o] if isr(o) else [], [i] if isr(i) else [])
        for o, i in pairs:
            if live:
                Q[e].dma_start(val_(o), val_(i)).then_inc(T.sem[s], 16)
            cnt[s] = cnt.get(s, 0) + 16
        note("dma", accs, (s, cnt[s]), e)

    def I_(w):
        return R(w, 16, 144)

    def SF(w):
        return R(w, 0, 128)

    def SBk(w):
        return R(w, 32, 160)

    def send(x, part):
        s, sb, sc, rb, rc, lb, lc = EX[x]
        if part == 0:
            deps("g", [], [R(sb, sc, sc + NR)])
            calls = [[(helper_of(T, topo, rank, k, rel), "ar", sc + k * X, T[rb][:, rc:rc + X]) for k in range(len(rel))]]
        else:
            deps("g", [], [R(sb, sc + NR, sc + E)])
            al = [(T.cores[(rank + s * d) % N], "ad", sc + NR + k * X, T[lb][:, lc[d]:lc[d] + X]) for k, d in enumerate(dirc)]
            calls = [al[k:k + 2] for k in range(0, len(al), 2)]
        for call in calls:
            tr = []
            for k, (dst, sm, c0, ap) in enumerate(call):
                es = topo.engines(core, dst)
                per = len(es) // len(call)
                rid, pid = topo.addr(dst, core)
                tr.append(RemoteDMATransfer(dst_ids=[DstId(rid=rid, pnc=pid)], dma_engine_mask=bits(es[k * per:(k + 1) * per]),
                                            remote_sem=T.sem[sm + str(x)], src=T[sb][:, c0:c0 + X], dst=ap))
                cnt["snt"] = cnt.get("snt", 0) + per
            if live:
                g.remote_dma_fused(tr, local_sem=T.sem.snt)

    noff = len(topo.engines(core, T.cores[(rank + dirc[0]) % N]))
    for x, (s, sb, sc, rb, rc, lb, lc) in enumerate(EX):
        cnt["ar%d" % x] = noff * len(rel)
        cnt["ad%d" % x] = noff * ((len(dirc) + 1) // 2)
        for d in order:
            nm = ("ar%d" if d in rel else "ad%d") % x
            log.setdefault(lb, []).append((lc[d], lc[d] + X, True, "r", (nm, cnt[nm]), 1))
    PARTS = ((0, 0, NR, 0, CR), (1, NR, E, CR, 35))

    def shifted(name, t, up):
        if up:
            return [(R(name, ap=T[name][16:128]), t[0:112]), (R(name, ap=T[name][0:16]), t[112:128])]
        return [(R(name, 16, 528, ap=T[name][0:112, 16:528]), t[16:128]), (R(name, 16, 528, ap=T[name][112:128, 16:528]), t[0:16])]
    dmas("s", "l1", shifted("dbf", T.debt, True))
    dmas("a", "l0", shifted("xf3", T.xpt, True))
    dmas("a", "l2", [(R("src", 0, 128), T.sig[:]), (R("src", 128, 163), T.xpt[:])])
    dmas("s", "l4", [(R("db"), T.debt[:])])
    dmas("s", "l3", [(R("col"), T.coll[:])])
    dmas("s", "l5", [(R("csh"), T.cash[:])])
    iota(R("io"), [[1, 992]], 64, 0, True)
    iota(R("it"), [[1, 160]], 240, -1)
    ms(R("zt"), 0.0)
    ts(R("xfU", 0, CR), R("xf3", ap=T.xf3[:, srel, :]), 0.25, A.mult, -0.375, A.add)
    ts(R("xfU", CR, 35), R("xf3", ap=T.xf3[:, sdir, :]), 0.25, A.mult, -0.375, A.add)
    ts(R("exh", 0, NR), G(R("dbf"), R("xfU", 0, CR)), 0.25, A.mult, -128.0, A.add)
    act(R("exh", NR, E), G(R("dbf"), R("xfU", CR, 35)), F.Copy, -128.0, 0.25)
    send(0, 0)
    send(0, 1)
    dmas("s", "dz", [(R("invA", ap=T.invA[0:128:16, 0:2608]), R("zt", 0, 163)),
                     (R("invB", 0, 2608, ap=T.invB[0:128:16, 0:2608]), R("zt", 0, 163))])
    dmas("s", "l6", [(R("thi", 0, 1), T.th[:])])
    C1, C2, C3, C4 = 62, 108, 130, 144
    iota(R("io2"), [[1, 16 * (163 - C3)]], 64 + 16 * C3, 0, True)
    iota(R("it2"), [[16, 10], [0, 16]], 255, -1)
    iota(R("it3"), [[1, 256]], 128, -1)
    iota(R("irow"), [[1, 128]], 0, 0, True)
    s163, s128 = R("src", 0, 163), R("src", 0, 128)
    ts(R("j1", 0, 163), s163, 8, A.arith_shift_right)
    ts(R("j2", 0, 128), s128, 4, A.arith_shift_right)
    ts(R("g1", 0, 163), s163, 8.0, A.mult)
    ts(R("g3", 0, 128), s128, 35.0, A.mult)
    ts(R("g2", 0, 163), R("j1", 0, 163), -2047.0, A.mult)
    ts(R("g4", 0, 128), R("j2", 0, 128), -559.0, A.mult, 1920.0, A.add)
    tt(R("g1", 0, 163), R("g1", 0, 163), R("g2", 0, 163), A.add)
    tt(R("g3", 0, 128), R("g3", 0, 128), R("g4", 0, 128), A.add)
    ts(R("g2", 0, 128), s128, 2048.0, A.is_ge)
    ts(R("j1", 0, 128), s128, 2, A.arith_shift_right)
    tt(R("g3", 0, 128), R("g3", 0, 128), R("g2", 0, 128), A.mult)
    ts(R("g4", 0, 128), s128, -1536.0, A.add)
    tt(R("g1", 0, 128), R("g1", 0, 128), R("g3", 0, 128), A.max)
    ts(R("it"), R("it"), 127, A.bitwise_and)
    cp(R("spU", 0, 163), R("g1", 0, 163))
    act(R("Lw", 0, 512), R("db"), F.Copy, -128.0, 0.25)
    act(R("e16"), R("csh"))
    act(G(R("invB", 0, 2608), R("spU", 0, C1)), R("io", 0, 16 * C1), F.Silu)
    tt(R("g2", 0, 128), R("g4", 0, 128), R("j1", 0, 128), A.max)
    ts(R("W1"), R("it"), 0.0, A.is_equal)
    cp(R("atU"), R("g2", 0, 128))
    ts(R("Wq"), R("it"), 0.0, A.is_equal, 0.25, A.mult)
    ts(R("cp"), R("col"), -128.0, A.add)

    def build_cp(qs):
        for q in qs:
            mm(R("q%d" % q), I_("W1"), R("cp", 512 * q, 512 * q + 512), True)
    build_cp((2, 3, 0, 1))
    ts(R("g2", 0, 128), R("g2", 0, 128), 4096.0, A.mult)
    ts(R("W1f"), R("it"), 0.0, A.is_equal)
    tt(R("wrS"), R("g2", 0, 128), R("g1", 0, 128), A.add)
    ts(R("Wn"), R("W1"), -1.0, A.mult)
    ts(G(R("invA"), R("spU", C1, C2)), R("io", 0, 16 * (C2 - C1)), 1.0, A.mult, 16.0 * C1, A.add)

    def convert(x, win):
        base = EX[x][2]
        ks = list(range(len(order)))
        for k in ks[1::2][::-1] + ks[0::2]:
            d = order[k]
            o, i = R(win, 512 + X * (d - 1), 512 + X * d), R("lnd", base + X * k, base + X * (k + 1))
            if k % 2:
                act(o, i)
            else:
                cp(o, i)

    CH = [("F", 0, 384), ("P", 1024, 1280), ("F", 384, 768), ("P", 1280, 1536), ("F", 768, 1024), ("P", 1536, 1792),
          ("P", 1792, 2048)]
    SPL = 384

    def sweep(win, wy, between):
        w = R(win)
        ps = [c for c in CH if c[0] == "P"]
        for n, (kind, a, b) in enumerate(CH):
            if n < len(ps):
                _, c, d = ps[n]
                act(R("xg", c - 1024, d - 1024), G(w, R("atU", c // 16, d // 16)))
            between(n)
            if kind == "F":
                tt(R("y", a, b), G(w, R("atU", a // 16, b // 16)), R("cp", a, b), A.max)
            else:
                tt(R("y", a, b), R("xg", a - 1024, b - 1024), R("q%d" % (a // 512), a % 512, (b - 1) % 512 + 1), A.max)
            o = R("sA", a // 4, b // 4) if b // 4 <= SPL else R("sB", a // 4 - SPL, b // 4 - SPL)
            for k in range(4):
                mm(o, wy, R("y", a + k, b, 4))

    mm(R("sA", 0, SPL), SF("Wq"), R("e16", 0, SPL), True)
    mm(R("sB", 0, V - SPL), SF("Wq"), R("e16", SPL, V), True)
    convert(0, "Lw")
    sweep("Lw", SF("Wq"), lambda n: None)
    act(G(R("invB", 0, 2608), R("spU", C3, C4)), R("io2", 0, 16 * (C4 - C3)), F.Silu)
    act(R("S1f", 0, SPL), R("sA", 0, SPL))
    cp(R("S1f", SPL, V), R("sB", 0, V - SPL))

    def lists(t):
        r = 3 - t
        cp(R("wWp", 0, CR), R("wW3", ap=T.wW3[:, srel, :]))
        cp(R("wWp", CR, 35), R("wW3", ap=T.wW3[:, sdir, :]))
        ts(R("wcU", 0, 35), R("wWp", 0, 35), -62.5, A.add)
        mm(R("pY", 0, 35), SBk("W1f"), R("wWp", 0, 35), True)
        act(R("cW", 0, NR), G(R("col"), R("wcU", 0, CR)), F.Copy, -128.0)
        ts(R("cW", NR, E), G(R("col"), R("wcU", CR, 35)), -128.0, A.add)
        ts(R("wbU", 0, 35), R("pY", 0, 35), 0.25, A.mult)

    def lists2(t):
        r = 3 - t
        if t < RO:
            ts(R("alU"), R("wrP", 32 * r, 32 * r + 32), 2111.0, A.min, 0.25, A.mult)
            cp(R("wc"), R("alU", 0, 8))

    offs = [sum(128 - 16 * c2 for c2 in range(c)) for c in range(9)]
    DL = (1536.0, 1664.0, 2096.0, 2224.0)

    for t in range(RO + 1):
        r = 3 - t
        close = t == RO
        xF, xB, xC = 1 + 3 * t, 2 + 3 * t, 3 + 3 * t
        sc = EX[xF][2]
        for part, a, b, ca, cb in PARTS:
            tt(R("exh", sc + a, sc + b), G(R("S1f", 0, V), R("xfU", ca, cb)), R("exh", a, b), A.min)
            send(xF, part)
        mm(R("pX"), SBk("W1f"), R("S1f", 0, V), True)
        if t:
            build_cp((0, 1))
        rowW = [(R("wW3", ap=T.wW3[:]), R("invB", ap=T.invB[0:128:16, 2048:2608]))]
        rowP = [(R("wrP"), R("invB", ap=T.invB[0:128:16, 0:2048]))]
        if t == 0:
            for nm in ("Dn", "m1b", "m1u", "h0", "h1", "h2", "vlb", "m1f"):
                iota(R(nm, 0, 16), [[0, 16]], 0, 0, True)
            iota(R("m1u", 528, 544), [[0, 16]], 0, 0, True)
            iota(R("sgx"), [[0, 8], [1024, 16]], -512, 0, True)
            act(G(R("invB", 0, 2608), R("spU", C4, 163)), R("io2", 16 * (C4 - C3), 16 * (163 - C3)), F.Silu)
            ts(G(R("invA"), R("spU", C2, C3)), R("io", 0, 16 * (C3 - C2)), 1.0, A.mult, 16.0 * C2, A.add)
            dmas("s", "dW", [(R("wW3", ap=T.wW3[:]), R("invA", ap=T.invA[0:128:16, 2048:2608]))])
            dmas("a", "dW2", [(R("wX3", ap=T.wX3[:]), rowW[0][1])])
            dmas("s", "dP", [(R("wrP"), R("invA", ap=T.invA[0:128:16, 0:2048]))])
            dmas("a", "dP2", [(R("wrP2"), rowP[0][1])])
            dmas("s", "l7", [(R("vl"), T.val[:])] + shifted("vlb", T.val, False))
            tt(R("xw", 0, V), R("pX"), R("Lw", 0, V), A.min)
            act(R("L16"), R("db"), F.Copy, -512.0)
            ts(R("it3"), R("it3"), 15, A.bitwise_and)
            ts(R("it2"), R("it2"), 127, A.bitwise_and)
            ts(R("mk"), R("it3"), 0.0, A.is_equal)
            ms(R("sg1"), 1.0)
            ts(R("B1f"), R("it2"), 16.0, A.is_lt)
            act(R("Wnq"), R("W1f"), F.Copy, 0.0, -0.25)
            act(R("W4"), R("W1f"), F.Copy, 0.0, 4.0)
            act(R("Wk"), R("W1f"), F.Copy, 0.0, -8192.0)
            act(R("mneg"), R("mk", 0, 128), F.Copy, -256.0, 247.5)
            act(R("Bn2"), R("B1f"), F.Copy, 0.0, -2.0)
            act(R("B1"), R("B1f"))
            act(R("Bk"), R("B1f"), F.Copy, 0.0, -8192.0)
            act(R("Bk32"), R("B1f"), F.Copy, 0.0, 32.0 * 8192)
            ms(R("sg1", 0, 256, 16), 0.0)
            tt(R("kt", 0, 128), R("irow"), R("mk", 0, 128), A.mult)
            ms(R("sgn"), -1e9)
            scan(R("kt2", 0, 128), R("sg1", 0, 128), R("kt", 0, 128), A.mult, A.add)
            ts(R("thc", 0, 1), R("thi", 0, 1), -16.0, A.add)
            cp(R("ncol"), R("kt2", 15, 128, 16))
            tt(R("j1", 0, 35), R("wW3", ap=T.wW3[:]), R("wX3", ap=T.wX3[:]), A.add)
            ts(R("wW3", ap=T.wW3[:]), R("j1", 0, 35), -1.5, A.add)
            lists(t)
        else:
            u8 = R("sB", 0, 8)
            for j in (0, 1):
                tt(R("o2", 8 * j, 8 * j + 8), u8, R("ub", 8 * j, 8 * j + 8), A.max)
            for j in (0, 1):
                ts(R("ouU", 8 * j, 8 * j + 8), R("o2", 8 * j, 8 * j + 8), DL[j], A.add)
            cp(G(R("sigr"), R("ouU", 0, 16)), R("AB"))
            dmas("s", "dS", [(R("wrS"), R("sigr", ap=T.sigr[0:128:16, 0:2048]))])
            ts(R("ok40", 128 * (t - 1), 128 * t), R("sA", 0, 128), -8.5 * 8192, A.is_lt, -40.0, A.mult)
            tt(R("xw", 0, V), R("pX"), R("Lw", 0, V), A.min)
            lists(t)
            ts(R("atU"), R("wrS"), 1.0 / 4096, A.mult, -0.32, A.add)
            lists2(t)
            if close:
                act(R("vW", 0, NR), G(R("vlb"), R("wbU", 0, CR)))
                cp(R("vW", NR, E), G(R("vlb"), R("wbU", CR, 35)))

        def pre(oa, ob, spl, pick):
            for o, a, b in ((oa, 0, spl), (ob, spl, V)):
                if a == b:
                    continue
                mm(R(o, 0, b - a), pick("W1"), R("L16", a, b), True)
                mm(R(o, 0, b - a), pick("Wn"), R("e16", a, b))
                for t2 in range(t):
                    mm(R(o, 3 - t2, b - a, 4), pick("W1"), R("ok40", 128 * t2 + a // 4, 128 * t2 + b // 4))
        pre("sA", "sB", SPL, SBk)
        mm(R("pX", 0, NR), SBk("Wn"), R("cW", 0, NR), True)
        mm(R("pY", 0, E - NR), SBk("Wn"), R("cW", NR, E), True)
        mm(R("pY", 0, E - NR), SBk("W1"), R("lnd", sc + NR, sc + E))
        mm(R("pX", 0, NR), SBk("W1"), R("lnd", sc, sc + NR))
        convert(xF, "xw")

        def between(n):
            if n == 1:
                act(R("MW", 0, NR), R("pX", 0, NR), F.Relu, 0.0, 8192.0)
            if n == 3:
                act(R("MW", NR, E), R("pY", 0, E - NR), F.Relu, 0.0, 8192.0)
        sweep("xw", SBk("Wn"), between)
        act(R("Dn", 16, 16 + SPL), R("sA", 0, SPL), F.Relu, 2.0 ** 23, -(2.0 ** 28))
        ts(R("Dn", 16 + SPL, 16 + V), R("sB", 0, V - SPL), 0.0, A.is_le, 2.0 ** 23, A.mult)
        sc = EX[xB][2]
        for part, a, b, ca, cb in PARTS:
            gd = G(R("Dn", 0, 528), R("wbU", ca, cb))
            if not close:
                tt(R("exb", sc + a, sc + b), gd, R("MW", a, b), A.is_lt)
            else:
                tt(R("c01w", a, b), gd, R("MW", a, b), A.is_lt)
                tt(R("exf", sc + a, sc + b), R("c01w", a, b), R("vW", a, b), A.mult)
            send(xB, part)
        cwn = "c%d" % t

        def bound(q):
            if q >= 2:
                build_cp((q,))
            for k in range(4):
                mm(R("q%d" % q, k, 512, 4), SF("W1"), R("Dn", 16 + 128 * q, 144 + 128 * q))

        def c01(q):
            tt(R(cwn, 512 * q, 512 * q + 512), R("y", 512 * q, 512 * q + 512), R("q%d" % q), A.is_gt)

        def names(cs):
            for c in cs:
                a, b = offs[c], offs[c + 1]
                ts(R("tb", a, b), R("Wr", 16 * c, 128), R("wc", c, c + 1), A.is_equal)

        def names_s():
            act(R("ng", 0, 8), R("vc"), F.Copy, 0.0, -1.0)
            act(R("ng", 8, 16), R("wc"), F.Copy, 0.0, -1.0)
            for c in range(8):
                a, b = offs[c], offs[c + 1]
                act(R("td", a, b), R("Wr", 16 * c, 128), F.Abs, R("ng", c, c + 1))
                act(R("td", 576 + a, 576 + b), R("Vr", 16 * c, 128), F.Abs, R("ng", 8 + c, 9 + c))

        def pre_e():
            for o, a in (("sA", 0), ("sB", 256)):
                mm(R(o, 0, 256), I_("Wn"), R("Dn", 16 + a, 272 + a), True)
                if close:
                    mm(R(o, 0, 256), I_("W1f"), R("vlb", 16 + a, 272 + a))
        if t == 0:
            tt(R("j2", 0, 128), R("wrP"), R("wrP2"), A.add)
            ts(R("wrP"), R("j2", 0, 128), -1.5, A.add)
            lists2(t)
            dmas("s", "dU", [(rowP[0][1], R("wrP")), (rowW[0][1], R("wW3", ap=T.wW3[:]))])
            dmas("s", "du", [(R("sigr", ap=T.sigr[j:128:16, 0:2048]), R("wrS")) for j in range(16)])
        if close:
            bound(0)
            bound(1)
            mm(R("pX"), I_("W1f"), R("vl"), True)
            bound(2)
            bound(3)
            pre_e()
            act(R("Wqf"), R("W1f"), F.Copy, 0.0, 0.25)
            ts(R("poU"), R("wrP"), -62.5, A.add)
            for q in range(4):
                c01(q)
            for k in range(4):
                tt(R("cf0", k, 2048, 4), R("c3", k, 2048, 4), R("pX"), A.mult)
        else:
            def spread():
                for c in range(8):
                    act(R("Em", 16 * c, 16 * c + 16), R("mk", 0, 16), F.Copy, 0.0, R("wc", c, c + 1))

            def spread2():
                mm(R("sA", 0, 128), I_("B1f"), R("Em"), True)
            if t:
                spread()
            act(R("Vr"), R("irow"), F.Copy, r + 16.0, 4.0)
            bound(0)
            for k in range(4):
                mm(R("pX", 128 * k, 128 * k + 128), I_("W1"), R("y", 4 * r + k, 2048, 16), True)
                mm(R("pX", 128 * k, 128 * k + 128), I_("Wn"), R("cp", 4 * r + k, 2048, 16))
            if t:
                spread2()
            act(R("sg"), R("pX"), F.Sign, -1.0 / 32)
            bound(1)
            mm(R("pY"), I_("Bn2"), R("sg"), True)
            if not t:
                spread()
                spread2()
            act(R("Wr"), R("sA", 0, 128))
            act(R("vb", 0, 128), R("sA", 0, 128), F.Copy, 1.5, 4.0)
            bound(2)
            for k in range(3):
                act(R("kt", 128 * k, 128 * k + 128), R("pY", 128 * k, 128 * k + 128), F.Copy, 3.0 - k)
            ts(R("wcl"), R("wc"), 527.0, A.min, -16.0, A.add)
            act(R("vc"), R("ncol"), F.Copy, r + 16.0, 4.0)
            act(R("abb", 0, 8), R("ncol"), F.Copy, 4.0 * r + 3, 16.0)
            act(R("abb", 8, 16), R("wcl"), F.Copy, 3.0, 4.0)
            act(R("vb", 128, 256), R("irow"), F.Copy, 4 * r + 65.5, 16.0)
            ts(R("poU"), R("wrP"), -62.5, A.add)
            names_s()
            c01(0)
            bound(3)
            mm(R("pX", 0, 8), SF("W1f"), R("wcl"), True)
            pre_e()
            act(R("bf", 8, 16), R("pX", 0, 8), F.Copy, -128.0)
            act(R("bf", 0, 8), R("vc"), F.Copy, -16.0)
            names((0,))
            c01(1)
            tt(R("pY", 0, 128), R("pY", 384, 512), R("kt", 0, 128), A.max)
            names((1,))
            tt(R("pY", 128, 256), R("pY", 0, 128), R("kt", 128, 256), A.max)
            c01(2)
            tt(R("key"), R("pY", 128, 256), R("kt", 256, 384), A.max)
            names((2,))
            ts(R("kk"), R("key"), 3, A.bitwise_and)
            c01(3)
            tt(R("kt", 0, 128), R("kk"), R("mk", 0, 128), A.mult)
            names((3,))
            scan(R("kw"), R("sg1", 0, 128), R("kt", 0, 128), A.mult, A.add)
            names((4,))
            tt(R("ab", 0, 8), R("abb", 0, 8), R("kw", 15, 128, 16), A.subtract)
            tt(R("ab", 8, 16), R("abb", 8, 16), R("kw", 15, 128, 16), A.subtract)
            cp(R("wU"), R("pX", 0, 8))
            ts(R("s1"), R("ab"), 4, A.arith_shift_right)
            ts(R("s2"), R("ab"), 128.0, A.mult)
            ts(R("s3"), R("s1"), -2047.0, A.mult)
            cp(R("abU"), R("ab"))
            tt(R("sgm"), R("s2"), R("s3"), A.add)
            cp(R("sgU"), R("sgm"))

        def threats(win, real, wz):
            zn, zsn = ("zf", "zsf") if real else ("z", "zs")
            w = R(win)

            def gat(a, b):
                return G(w, R("poU", a // 16, b // 16))

            def feed(src, a, rr):
                for o, i0 in (("sA", 0), ("sB", 64)):
                    mm(R(o, rr, 256, 4), wz, R(src, a + i0, a + i0 + 64))

            def fused(a, n):
                tt(R(zn, a, a + n), gat(a, a + n), R(zsn, a - 256, a - 256 + n), A.add)
            if real:
                act(R(zsn, 0, 128), gat(0, 128))
                act(R(zsn, 128, 256), gat(128, 256))
                for rr in range(1, 4):
                    act(R(zsn, 512 * rr, 512 * rr + 256), gat(512 * rr, 512 * rr + 256))

                def add(rr):
                    a = 512 * rr + 256
                    tt(R("tf", 128 * rr, 128 * rr + 128), R(zn, a, a + 128), R(zn, a + 128, a + 256), A.add)
                    feed("tf", 128 * rr, rr)
                fused(256, 128)
                feed(zn, 256, 0)
                fused(384, 128)
                feed(zn, 384, 0)
                fused(768, 256)
                fused(1280, 256)
                add(1)
                fused(1792, 256)
                add(2)
                add(3)
                return
            rest = [x for x in range(4) if x != r]
            for rr in rest:
                act(R(zsn, 512 * rr, 512 * rr + 256), gat(512 * rr, 512 * rr + 256))
            a = 512 * r
            act(R(zn, a, a + 256), gat(a, a + 256))
            cp(R(zn, a + 256, a + 512), gat(a + 256, a + 512))
            feed(zn, a + 256, r)
            feed(zn, a + 384, r)
            for rr in rest:
                fused(512 * rr + 256, 256)
                if rr == rest[-1]:
                    feed(zn, a, r)
                    feed(zn, a + 128, r)
                feed(zn, 512 * rr + 256, rr)
                feed(zn, 512 * rr + 384, rr)

        sc = EX[xC][2]
        if close:
            threats("cf0", True, SBk("Wqf"))
            act(R("m1f", 16, 272), R("sA", 0, 256), F.Relu)
            ts(R("m1f", 272, 528), R("sB", 0, 256), 0.0, A.max)
            for part, a, b, ca, cb in PARTS:
                tt(R("exf", sc + a, sc + b), G(R("m1f"), R("wbU", ca, cb)), R("MW", a, b), A.min)
                send(xC, part)
            mm(R("pX"), SF("W1f"), R("m1f", 16, 528), True)
            pre("pY", "pY", V, I_)
            for k in range(4):
                mm(R("pY"), I_("Wn"), R("y", k, 2048, 4))
            for o, a in (("sA", 0), ("sB", 256)):
                mm(R(o, 0, 256), SF("Wn"), R("Dn", 16 + a, 272 + a), True)
                mm(R(o, 0, 256), I_("W1f"), R("vl", a, a + 256))
            for k in range(4):
                tt(R("cf1", k, 2048, 4), R("c3", k, 2048, 4), R("pX"), A.mult)
            act(R("res", 0, V), R("pY"), F.Relu)
            tt(R("res", 0, V), R("db"), R("res", 0, V), A.subtract)
            dmas("s", "st1", [(T.pay[:], R("res", 0, V))])
            threats("cf1", True, I_("Wqf"))
            act(R("res2", 0, 256), R("sA", 0, 256), F.Relu)
            ts(R("res2", 256, 512), R("sB", 0, 256), 0.0, A.max)
            dmas("a", "st2", [(T.mu[:, 0:256], R("res2", 0, 256))])
            dmas("s", "l8", [(T.mu[:, 256:512], R("res2", 256, 512))])
            break
        threats(cwn, False, SBk("Wq"))
        act(R("m1b", 16, 272), R("sA", 0, 256), F.Relu, 1.0)
        ts(R("m1b", 272, 528), R("sB", 0, 256), 1.0, A.add, 0.0, A.max)
        for part, a, b, ca, cb in PARTS:
            tt(R("exb", sc + a, sc + b), G(R("m1b", 0, 528), R("wbU", ca, cb)), R("MW", a, b), A.min)
            send(xC, part)
        mm(R("pY"), SF("W1"), R("m1b", 16, 528), True)
        tt(R("ABm"), G(R("sigr", 0, 2048), R("sgU")), R("mk"), A.mult)
        act(R("tb", 576, 1728), R("td"), F.Relu, 1.0, -1.0)
        act(R("m1u", 16, 528), R("pY"))
        act(R("cab"), G(R("col"), R("abU")), F.Copy, -128.0)
        names((5,))
        scan(R("ABs"), R("sg1"), R("ABm"), A.mult, A.add)
        names((6, 7))
        if t == 0:
            ts(R("tri"), R("irow", 0, 16), R("ncol", 0, 1), A.is_le, -4.0, A.mult)
            ts(R("sgn", 0, 128, 16), R("ncol"), 512.0, A.add)
        ts(R("aaU"), R("ABs", 15, 256, 16), 1.0 / 4096, A.mult, -0.32, A.add)
        act(R("Xv"), G(R("Lw"), R("aaU")))
        act(R("S1w", 128, 256), G(R("S1f", 0, V), R("wU")))
        act(R("S1w", 0, 128), R("S1f", r, V, 4), F.Copy, 10.0)
        act(R("en1"), R("Wr"), F.Relu, -527.0)
        for o, a, b in (("sA", 0, 480), ("sB", 480, 576)):
            for j in range(3):
                mm(R(o, 0, b - a), I_("W1"), R("tb", 576 * j + a, 576 * j + b), j == 0)
            for c in range(8):
                if a <= offs[c] < b:
                    mm(R(o, offs[c] - a, offs[c] - a + 16), I_("W1"), R("tri"))
        mm(R("pY", 256, 512), I_("W1"), R("cab"), True)
        tt(R("en2"), R("Wr"), R("Vr"), A.is_equal)
        tt(R("zl"), G(R("m1u"), R("alU")), R("z", 512 * r, 512 * r + 512), A.mult)
        act(R("Bp", 0, 480), R("sA", 0, 480), F.Relu, 64.0, -64.0)
        act(R("Bp", 480, 576), R("sB", 0, 96), F.Relu, 64.0, -64.0)
        mm(R("pX", 0, 128), SF("Wn"), R("Dn", 16 + r, 528, 4), True)
        mm(R("pX", 0, 128), I_("Wk"), R("en1"))
        mm(R("pX", 0, 128), I_("Wk"), R("en2"))
        mm(R("q2", 0, 128), I_("W1"), R("mneg"), True)
        mm(R("q3", 0, 128), I_("Wk"), R("mneg"), True)
        for l in range(4):
            mm(R("pX", 0, 128), I_("W4"), R("zl", 128 * l, 128 * l + 128))
        ts(R("ahU"), R("wrP", 32 * r, 32 * r + 32), -62.5 - 2032.0, A.add, 15.0, A.max)
        tt(R("rl", 0, 256), R("Xv"), R("pY", 256, 512), A.max)
        tt(R("rl", 256, 384), R("Xv", 128, 256), R("pY", 256, 384), A.max)
        tt(R("rl", 384, 512), R("Xv", 0, 128), R("pY", 384, 512), A.max)
        mm(R("pY", 0, 256), SF("Wq"), R("rl", 256, 512), True)
        mm(R("pY", 0, 256), SF("Wnq"), R("rl", 0, 256))
        cp(R("ci"), R("ABs", 15, 256, 16))
        tt(R("vals", 128, 256), R("vb", 128, 256), R("kk"), A.subtract)
        tt(R("nv"), R("pY", 0, 256), R("S1w"), A.add)
        hw = R("h%d" % t)
        for l in range(4):
            o, i = R("zg", 128 * l, 128 * l + 128), G(hw, R("ahU", 8 * l, 8 * l + 8))
            if l % 2:
                act(o, i)
            else:
                cp(o, i)
            mm(R("pX", 0, 128), I_("W4"), o)
        tt(R("vals", 0, 128), R("vb", 0, 128), R("kk"), A.subtract)
        ts(R("vote"), R("pX", 0, 128), R("thc", 0, 1), A.is_ge)
        mm(R("q2", 0, 128), I_("B1"), R("vote"))
        mm(R("q3", 0, 128), SF("Bk"), R("vote"))
        act(R("AB"), G(R("sigr", 0, 2048), R("sgU")))
        ts(R("spo"), R("ci"), 4095, A.bitwise_and)
        ts(R("ub", 0, 8), R("sgm", 8, 16), -DL[0], A.add)
        scan(R("cw"), R("sgx"), R("q2", 0, 128), A.min, A.max)
        ts(R("ub", 8, 16), R("sgm", 0, 8), -DL[1], A.add)
        for c in range(8):
            a, b = offs[c], offs[c + 1]
            ts(R("tmp", a, b), R("Bp", a, b), R("cw", 16 * c + 15, 16 * c + 16), A.is_lt)
            mm(R("q3", 16 * c, 128), SF("Bk32"), R("tmp", a, b))
        ts(R("ub", 16, 24), R("spo", 0, 8), -DL[2], A.add)
        ts(R("ub", 24, 32), R("spo", 8, 16), -DL[3], A.add)
        scan(R("scw"), R("sgn"), R("q3", 0, 128), A.max, A.min)
        mm(R("sB", 0, 8), SBk("W1f"), R("scw", 15, 128, 16), True)
        mm(R("sA", 0, 128), I_("Bk"), R("vote"), True)
        for c in range(8):
            mm(R("sA", 16 * c, 128), I_("Bk32"), R("tmp", offs[c], offs[c + 1]))
        build_cp((2, 3))
        tt(R("o1", 0, 8), R("scw", 15, 128, 16), R("bf", 0, 8), A.max)
        tt(R("o1", 8, 16), R("scw", 15, 128, 16), R("bf", 8, 16), A.max)
        cp(R("ofU", 0, 8), R("o1", 0, 8))
        ts(R("ofU", 8, 16), R("o1", 8, 16), 128.0, A.add)
        for j in (2, 3):
            tt(R("o2", 8 * j, 8 * j + 8), R("sB", 0, 8), R("ub", 8 * j, 8 * j + 8), A.max)
        for j in (2, 3):
            ts(R("ouU", 8 * j, 8 * j + 8), R("o2", 8 * j, 8 * j + 8), DL[j], A.add)
        act(G(R("invB"), R("ouU", 16, 32)), R("vals"), F.Silu)
        dmas("a", "dW", rowW)
        dmas("a", "dP", rowP)
        cp(G(R("S1f"), R("ofU")), R("nv"))
    for s, n in cnt.items():
        wait("g", (s, n))
    return seq
